import numpy as np
import ml_dtypes


def mxq(x, axis, fmt="e4m3"):
    dtype, down = {"e4m3": (ml_dtypes.float8_e4m3fn, 7), "e5m2": (ml_dtypes.float8_e5m2, 14)}[fmt]
    v = np.moveaxis(np.asarray(x, np.float32).astype(ml_dtypes.bfloat16).astype(np.float64), axis, -1)
    blocks = v.reshape(v.shape[:-1] + (-1, 32))
    amax = np.abs(blocks).max(-1, keepdims=True)
    byte = np.maximum(np.where(amax > 0, np.frexp(amax)[1] - 1 + 127, 0) - down, 1)
    scale = np.exp2(byte - 127.0)
    codes = (blocks / scale).astype(np.float32).astype(dtype).astype(np.float64)
    return np.moveaxis((codes * scale).reshape(v.shape), -1, axis)


WIDE = False


def mx_kscale(k):
    if not WIDE:
        return np.ones(k)
    levels = np.array([10, -10, 5, -5, 0])
    if k % 512:
        return np.exp2(np.random.permutation(np.resize(levels, k // 32))).repeat(32)
    a = np.empty((k // 512, 16))
    for p in range(k // 512):
        a[p, :8] = np.random.permutation(np.resize(levels, 8))
        for g in range(8):
            far = levels[np.abs(levels - a[p, g]) >= 10]
            a[p, g + 8] = far[np.random.randint(len(far))]
    return np.exp2(a.ravel()).repeat(32)


def f64(x):
    return np.asarray(x).astype(np.float64)


def striped(idx):
    return np.tile(idx.reshape(-1, 16).T, (8, 1)).astype(np.uint16)


def unstriped(offs):
    return offs[:16].T.reshape(-1).astype(np.int64)


def striped8(idx):
    return np.concatenate([x.reshape(-1, 16).T for x in idx]).astype(np.uint16)


def runs(offs, k):
    lists = np.stack([offs[16 * r : 16 * r + 16].T.reshape(-1) for r in range(8)]).astype(np.int64)
    return lists[np.arange(k) % 512 // 64]


def pack_weight(w):
    k, n = w.shape
    w = f64(np.asarray(w, np.float32).astype(ml_dtypes.bfloat16)).reshape(k // 32, 32, n)
    amax = np.abs(w).max(1)
    byte = np.clip(np.where(amax > 0, np.frexp(amax)[1] - 1 + 127 - 7, 1), 1, 254)
    scaled = (w * np.exp2(127.0 - byte)[:, None, :]).reshape(k, n).astype(np.float32)
    words = np.ascontiguousarray(scaled.reshape(k // 512, 128, 4, n).transpose(0, 1, 3, 2)).astype(ml_dtypes.float8_e4m3fn).view(np.uint8)
    return words, np.ascontiguousarray(byte.astype(np.uint8).reshape(k // 512, 16, n))


def unpack_weight(words, scales):
    g, p, n, _ = words.shape
    vals = np.ascontiguousarray(words).view(ml_dtypes.float8_e4m3fn).astype(np.float64) * np.repeat(np.exp2(scales.astype(np.float64) - 127.0), 8, axis=1)[..., None]
    return vals.transpose(0, 1, 3, 2).reshape(g * 512, n)


E2M1 = np.array([0.0, 0.5, 1.0, 1.5, 2.0, 3.0, 4.0, 6.0, -0.0, -0.5, -1.0, -1.5, -2.0, -3.0, -4.0, -6.0])


def pack_fp4(w):
    k, n = w.shape
    w = f64(np.asarray(w, np.float32).astype(ml_dtypes.bfloat16)).reshape(k // 32, 32, n)
    amax = np.abs(w).max(1)
    mant, ex = np.frexp(amax / 6.0)
    byte = np.clip(np.where(amax > 0, np.where(mant > 0.5, ex, ex - 1) + 127, 1), 1, 254)
    scaled = (w * np.exp2(127.0 - byte)[:, None, :]).reshape(k, n).astype(np.float32)
    c = np.ascontiguousarray(scaled.reshape(k // 512, 128, 4, n).transpose(0, 1, 3, 2)).astype(ml_dtypes.float4_e2m1fn).view(np.uint8) & 0xF
    words = (c[..., 0::2] | (c[..., 1::2] << 4)).reshape(k // 512, 128, 2 * n)
    return np.ascontiguousarray(words), np.ascontiguousarray(byte.astype(np.uint8).reshape(k // 512, 16, n))


def unpack_fp4(words, scales):
    g, _, n = scales.shape
    words = np.ascontiguousarray(words).reshape(g, 128, n, 2)
    nib = np.empty((g, 128, n, 4), np.uint8)
    nib[..., 0::2] = words & 0xF
    nib[..., 1::2] = words >> 4
    vals = E2M1[nib] * np.repeat(np.exp2(scales.astype(np.float64) - 127.0), 8, axis=1)[..., None]
    return vals.transpose(0, 1, 3, 2).reshape(g * 512, n)


def planes(y):
    n, m = y.shape
    v = y.astype(np.float32).astype(ml_dtypes.bfloat16).astype(np.float64).reshape(n // 32, 32, m)
    top = np.abs(v).max(1)
    byte = np.clip(np.where(top > 0, np.frexp(top)[1] - 1 + 127 - 7, 1), 1, 254)
    codes = (v * np.exp2(127.0 - byte)[:, None, :]).reshape(n, m).astype(np.float32).astype(ml_dtypes.float8_e4m3fn).view(np.uint8)
    words = codes.reshape(n // 512, 128, 4, m).transpose(0, 1, 3, 2)
    return np.ascontiguousarray(words), np.ascontiguousarray(byte.astype(np.uint8).reshape(n // 512, 16, m))


K, T, S, N, H = 512, 2048, 512, 512, 512


def setup_inputs():
    n = np.random.standard_normal
    s = mx_kscale(K)[:, None]
    u = mx_kscale(S)
    packed_xT = pack_weight(n((K, T)) * s)
    packed_w1 = pack_fp4(n((S, N)) / np.sqrt(S) / u[:, None])
    return {
        "x_words": packed_xT[0],
        "x_scales": packed_xT[1],
        "wa": (n((K, H)) / np.sqrt(K) / s).astype(np.float32),
        "wb": (n((K, H)) / np.sqrt(K) / s).astype(np.float32),
        "gt": (np.random.uniform(0.5, 1.5, (S, 1)) * u[:, None]).astype(np.float32),
        "w1_words": packed_w1[0],
        "w1_scales": packed_w1[1],
        "offs": striped(np.random.permutation(T)[:S]),
        "two": striped(np.random.permutation(T)[:S]),
        "n1": striped8(np.stack([np.random.permutation(H) for _ in range(8)])),
        "n2": striped8(np.stack([np.random.permutation(H) for _ in range(8)])),
        "n3": striped8(np.stack([np.random.permutation(H) for _ in range(8)])),
        "n4": striped8(np.stack([np.random.permutation(H) for _ in range(8)])),
        "n5": striped8(np.stack([np.random.permutation(H) for _ in range(8)])),
    }


def reference(x_words, x_scales, wa, wb, gt, w1_words, w1_scales, offs, two, n1, n2, n3, n4, n5):
    x_two = unpack_weight(x_words, x_scales)[:, unstriped(two)]
    d = x_two.T @ mxq(f64(wb), 0, "e4m3")
    xq = unpack_weight(x_words, x_scales)[:, unstriped(offs)]
    y = xq.T @ mxq(f64(wa), 0, "e4m3")
    z = f64(gt) * (d * (y[np.arange(S)[:, None], runs(n1, S)] - y) + 0.5 * ((d[np.arange(S)[:, None], runs(n3, S)]) * (y[np.arange(S)[:, None], runs(n2, S)] - y)))
    h = unpack_fp4(w1_words, w1_scales).T @ mxq(z, 0, "e4m3")
    ex = np.exp(h)
    out_0 = np.log(ex + ex[np.arange(N)[:, None], runs(n4, N)]) - (h[np.arange(N)[:, None], runs(n5, N)])
    return (out_0,) + planes(out_0)

@@ -1,0 +1,223 @@
+from contextlib import ExitStack
+
+import concourse.mybir as mybir
+
+K, T, S, N, H = 512, 2048, 512, 512, 512
+FLOPS = 3 * 2 * 512 * 512 * 512
+
+F32 = mybir.dt.float32
+BF16 = mybir.dt.bfloat16
+I32 = mybir.dt.int32
+U32 = mybir.dt.uint32
+U16 = mybir.dt.uint16
+U8 = mybir.dt.uint8
+FP8X4 = mybir.dt.float8_e4m3fn_x4
+FP4X4 = mybir.dt.float4_e2m1fn_x4
+ALU = mybir.AluOpType
+ACT = mybir.ActivationFunctionType
+
+P = 128
+R = 4
+HALF = 256
+HALVES = ((0, 256), (256, 512))
+CHUNKS = ((0, 256), (256, 384), (384, 512))
+
+
+def tile_picked_twtflowblse_none_po_kernel(tc, x_words, x_scales, wa, wb, gt, w1_words, w1_scales, offs, two, n1, n2, n3, n4, n5, out_0, out_1, out_2):
+    nc = tc.nc
+
+    with ExitStack() as ctx:
+        lists = ctx.enter_context(tc.tile_pool(name="lists", bufs=1))
+        keep = ctx.enter_context(tc.tile_pool(name="keep", bufs=1))
+        psum = ctx.enter_context(tc.psum_pool(name="psum", bufs=4))
+
+        def load_list(src, name):
+            tile = lists.tile([P, 32], U16, name=name)
+            nc.sync.dma_start(tile[:], src)
+            return tile
+
+        def sb(shape, dtype, name):
+            return keep.tile(shape, dtype, name=name, align_bytes=64)
+
+        def entries(lst, c0, c1):
+            return lst[:, c0 // 16 : c1 // 16]
+
+        def load_scales(src, width, name):
+            plane = sb([P, width], U8, name)
+            nc.vector.memset(plane[:].bitcast(I32), 0)
+            for q in range(4):
+                nc.scalar.dma_start(plane[32 * q : 32 * q + 4, :].bitcast(I32), src[0, 4 * q : 4 * q + 4, :].bitcast(I32))
+            return plane
+
+        def load_weight(w, name):
+            halves = []
+            for u, (c0, c1) in enumerate(HALVES):
+                raw = sb([P, R, HALF], F32, "%s_raw%d" % (name, u))
+                nc.sync.dma_start(raw[:], w.rearrange("(p t) c -> p t c", t=R)[:, :, c0:c1])
+                halves.append(raw)
+            return halves
+
+        def interleave(engine_copy, dst, src):
+            engine_copy(dst.rearrange("p (c i t) -> p c t i", i=4, t=R), src.rearrange("p t (c i) -> p c t i", i=4))
+
+        def quantise_weight(halves, name):
+            grouped = sb([P, R * H], BF16, name + "_bf")
+            codes = sb([P, H], U32, name + "_codes")
+            scales = sb([P, H], U8, name + "_scales")
+            for raw, (c0, c1) in zip(halves, HALVES):
+                interleave(nc.scalar.copy, grouped[:, R * c0 : R * c1], raw[:])
+            nc.vector.quantize_mx(codes[:].bitcast(FP8X4), scales[:], grouped[:])
+            return codes, scales
+
+        xs = load_scales(x_scales, T, "xs")
+        l_offs = load_list(offs, "l_offs")
+        l_two = load_list(two, "l_two")
+        xw = sb([P, T], U32, "xw")
+        nc.sync.dma_start(xw[:].bitcast(I32), x_words[0].rearrange("p n t -> p (n t)").bitcast(I32))
+        wa_raw = load_weight(wa, "wa")
+        wb_raw = load_weight(wb, "wb")
+        l_n1 = load_list(n1, "l_n1")
+        l_n2 = load_list(n2, "l_n2")
+        w1w = sb([P, 2 * N], U8, "w1w")
+        nc.sync.dma_start(w1w[:].bitcast(I32), w1_words[0].bitcast(I32))
+        w1s = load_scales(w1_scales, N, "w1s")
+        gate = sb([P, R], F32, "gate")
+        nc.sync.dma_start(gate[:], gt.rearrange("(p t) o -> p (t o)", t=R))
+        l_n3 = load_list(n3, "l_n3")
+        l_n4 = load_list(n4, "l_n4")
+        l_n5 = load_list(n5, "l_n5")
+
+        def pick_scales(lst, name):
+            picked = sb([P, S], U8, name + "_sg")
+            nc.vector.tensor_copy(picked[:], xs[:].indirect(lst[:]))
+            dealt = sb([P, S], U8, name + "_sd")
+            nc.vector.tensor_copy(
+                dealt[:].rearrange("p (t c i) -> p c t i", t=R, i=16),
+                picked[:].rearrange("p (c i t) -> p c t i", t=R, i=16),
+            )
+            return dealt
+
+        def pick_words(lst, name):
+            picked = sb([P, S], U32, name + "_g")
+            nc.vector.tensor_copy(picked[:], xw[:].indirect(lst[:]))
+            dealt = sb([P, S], U32, name + "_d")
+            nc.vector.tensor_copy(
+                dealt[:].rearrange("p (t c i) -> p c t i", t=R, i=4),
+                picked[:].rearrange("p (c i t) -> p c t i", t=R, i=4),
+            )
+            return dealt
+
+        def project(words, word_scales, codes, scales, t):
+            acc = psum.tile([P, H], F32, name="acc")
+            nc.tensor.matmul_mx(
+                acc[:],
+                lhsT=words[:, P * t : P * (t + 1)].bitcast(FP8X4),
+                lhsT_scale=word_scales[:, P * t : P * (t + 1)],
+                rhs=codes[:].bitcast(FP8X4),
+                rhs_scale=scales[:],
+                start=True,
+                stop=True,
+            )
+            return acc
+
+        xa_s = pick_scales(l_offs, "xa")
+        xb_s = pick_scales(l_two, "xb")
+        xa = pick_words(l_offs, "xa")
+        wa_codes, wa_scales = quantise_weight(wa_raw, "wa")
+        xb = pick_words(l_two, "xb")
+
+        w1w_d = sb([P, 2 * N], U8, "w1w_d")
+        nc.vector.tensor_copy(
+            w1w_d[:].rearrange("p (t c i b) -> p c t i b", t=R, i=8, b=2),
+            w1w[:].rearrange("p (c i t b) -> p c t i b", t=R, i=8, b=2),
+        )
+        w1s_d = sb([P, N], U8, "w1s_d")
+        nc.vector.tensor_copy(
+            w1s_d[:].rearrange("p (t c i) -> p c t i", t=R, i=16),
+            w1s[:].rearrange("p (c i t) -> p c t i", t=R, i=16),
+        )
+
+        y_win = [sb([P, H], F32, "y_win%d" % t) for t in range(R)]
+        y_pl = [sb([P, H], F32, "y_pl%d" % t) for t in range(R)]
+        diff1 = [sb([P, H], F32, "diff1_%d" % t) for t in range(R)]
+        diff2 = [sb([P, H], F32, "diff2_%d" % t) for t in range(R)]
+        for t in range(R):
+            acc = project(xa, xa_s, wa_codes, wa_scales, t)
+            nc.scalar.copy(y_win[t][:], acc[:])
+            nc.scalar.copy(y_pl[t][:], acc[:])
+
+        def differences(c0, c1):
+            for t in range(R):
+                nc.vector.tensor_tensor(diff1[t][:, c0:c1], y_win[t][:].indirect(entries(l_n1, c0, c1)), y_pl[t][:, c0:c1], ALU.subtract)
+                nc.vector.tensor_tensor(diff2[t][:, c0:c1], y_win[t][:].indirect(entries(l_n2, c0, c1)), y_pl[t][:, c0:c1], ALU.subtract)
+
+        differences(*HALVES[0])
+        wb_codes, wb_scales = quantise_weight(wb_raw, "wb")
+        differences(*HALVES[1])
+
+        d_win = [sb([P, H], F32, "d_win%d" % t) for t in range(R)]
+        for t in range(R):
+            acc = project(xb, xb_s, wb_codes, wb_scales, t)
+            nc.scalar.activation(d_win[t][:], acc[:], ACT.Copy, scale=gate[:, t : t + 1])
+
+        ex_win = [sb([P, H], F32, "ex_win%d" % t) for t in range(R)]
+        ex_pl = [sb([P, H], F32, "ex_pl%d" % t) for t in range(R)]
+        nh_win = [sb([P, H], F32, "nh_win%d" % t) for t in range(R)]
+        for k, (c0, c1) in enumerate(CHUNKS):
+            w = c1 - c0
+            term1 = sb([P, R, w], F32, "term1_%d" % k)
+            term2 = sb([P, R, w], F32, "term2_%d" % k)
+            z = sb([P, R, w], F32, "z%d" % k)
+            for t in range(R):
+                nc.vector.tensor_tensor(term1[:, t, :], diff1[t][:, c0:c1], d_win[t][:, c0:c1], ALU.mult)
+            for t in range(R):
+                nc.vector.tensor_tensor(term2[:, t, :], d_win[t][:].indirect(entries(l_n3, c0, c1)), diff2[t][:, c0:c1], ALU.mult)
+            flat = "p t c -> p (t c)"
+            nc.vector.scalar_tensor_tensor(z[:].rearrange(flat), term2[:].rearrange(flat), 0.5, term1[:].rearrange(flat), ALU.mult, ALU.add)
+            z_bf = sb([P, R * w], BF16, "z_bf%d" % k)
+            interleave(nc.vector.tensor_copy if k == len(CHUNKS) - 1 else nc.scalar.copy, z_bf[:], z[:])
+            z_codes = sb([P, w], U32, "z_codes%d" % k)
+            z_scales = sb([P, w], U8, "z_scales%d" % k)
+            nc.vector.quantize_mx(z_codes[:].bitcast(FP8X4), z_scales[:], z_bf[:])
+            for t in range(R):
+                hacc = psum.tile([P, H], F32, name="hacc")
+                nc.tensor.matmul_mx(
+                    hacc[:, 0:w],
+                    lhsT=w1w_d[:, 2 * P * t : 2 * P * (t + 1)].bitcast(FP4X4),
+                    lhsT_scale=w1s_d[:, P * t : P * (t + 1)],
+                    rhs=z_codes[:].bitcast(FP8X4),
+                    rhs_scale=z_scales[:],
+                    start=True,
+                    stop=True,
+                )
+                nc.scalar.activation(ex_win[t][:, c0:c1], hacc[:, 0:w], ACT.Exp)
+                nc.scalar.activation(ex_pl[t][:, c0:c1], hacc[:, 0:w], ACT.Exp)
+                nc.scalar.activation(nh_win[t][:, c0:c1], hacc[:, 0:w], ACT.Copy, scale=-1.0)
+
+        logs = []
+        for u, (c0, c1) in enumerate(HALVES):
+            both = sb([P, R, HALF], F32, "both%d" % u)
+            for t in range(R):
+                nc.vector.tensor_tensor(both[:, t, :], ex_win[t][:].indirect(entries(l_n4, c0, c1)), ex_pl[t][:, c0:c1], ALU.add)
+            lg = sb([P, R, HALF], F32, "lg%d" % u)
+            nc.scalar.activation(lg[:], both[:], ACT.Ln)
+            logs.append(lg)
+
+        o_scales = sb([P, H], U8, "o_scales")
+        out_rows = out_0.rearrange("(p t) c -> p t c", t=R)
+        out_words = out_1[0].rearrange("p c t -> p (c t)").bitcast(I32)
+        for k, (c0, c1) in enumerate(CHUNKS):
+            w = c1 - c0
+            lg = logs[c0 // HALF]
+            o = sb([P, R, w], F32, "o%d" % k)
+            for t in range(R):
+                nc.vector.tensor_tensor(o[:, t, :], nh_win[t][:].indirect(entries(l_n5, c0, c1)), lg[:, t, c0 % HALF : c0 % HALF + w], ALU.add)
+            nc.sync.dma_start(out_rows[:, :, c0:c1], o[:])
+            o_bf = sb([P, R * w], BF16, "o_bf%d" % k)
+            interleave(nc.vector.tensor_copy if k == len(CHUNKS) - 1 else nc.scalar.copy, o_bf[:], o[:])
+            o_codes = sb([P, w], U32, "o_codes%d" % k)
+            nc.vector.quantize_mx(o_codes[:].bitcast(FP8X4), o_scales[:, c0:c1], o_bf[:])
+            nc.sync.dma_start(out_words[:, c0:c1], o_codes[:].bitcast(I32))
+        for q in range(4):
+            queue = nc.scalar if q % 2 else nc.sync
+            queue.dma_start(out_2[0, 4 * q : 4 * q + 4, :].bitcast(I32), o_scales[32 * q : 32 * q + 4, :].bitcast(I32))

@@ -1,6 +1,7 @@
 from contextlib import ExitStack
 
 import concourse.mybir as mybir
+from concourse.masks import make_identity
 
 K, T, S, N, H = 512, 2048, 512, 512, 512
 FLOPS = 3 * 2 * 512 * 512 * 512
@@ -21,6 +22,7 @@ R = 4
 HALF = 256
 HALVES = ((0, 256), (256, 512))
 CHUNKS = ((0, 256), (256, 384), (384, 512))
+SCALAR_UNITS = 3
 
 
 def tile_picked_twtflowblse_none_po_kernel(tc, x_words, x_scales, wa, wb, gt, w1_words, w1_scales, offs, two, n1, n2, n3, n4, n5, out_0, out_1, out_2):
@@ -29,7 +31,7 @@ def tile_picked_twtflowblse_none_po_kernel(tc, x_words, x_scales, wa, wb, gt, w1
     with ExitStack() as ctx:
         lists = ctx.enter_context(tc.tile_pool(name="lists", bufs=1))
         keep = ctx.enter_context(tc.tile_pool(name="keep", bufs=1))
-        psum = ctx.enter_context(tc.psum_pool(name="psum", bufs=4))
+        psum = ctx.enter_context(tc.psum_pool(name="psum", bufs=1))
 
         def load_list(src, name):
             tile = lists.tile([P, 32], U16, name=name)
@@ -42,11 +44,11 @@ def tile_picked_twtflowblse_none_po_kernel(tc, x_words, x_scales, wa, wb, gt, w1
         def entries(lst, c0, c1):
             return lst[:, c0 // 16 : c1 // 16]
 
-        def load_scales(src, width, name):
+        def load_scales(queue, src, width, name):
             plane = sb([P, width], U8, name)
             nc.vector.memset(plane[:].bitcast(I32), 0)
             for q in range(4):
-                nc.scalar.dma_start(plane[32 * q : 32 * q + 4, :].bitcast(I32), src[0, 4 * q : 4 * q + 4, :].bitcast(I32))
+                queue.dma_start(plane[32 * q : 32 * q + 4, :].bitcast(I32), src[0, 4 * q : 4 * q + 4, :].bitcast(I32))
             return plane
 
         def load_weight(w, name):
@@ -69,46 +71,43 @@ def tile_picked_twtflowblse_none_po_kernel(tc, x_words, x_scales, wa, wb, gt, w1
             nc.vector.quantize_mx(codes[:].bitcast(FP8X4), scales[:], grouped[:])
             return codes, scales
 
-        xs = load_scales(x_scales, T, "xs")
+        xs = load_scales(nc.scalar, x_scales, T, "xs")
         l_offs = load_list(offs, "l_offs")
         l_two = load_list(two, "l_two")
+        l_n1 = load_list(n1, "l_n1")
+        l_n2 = load_list(n2, "l_n2")
         xw = sb([P, T], U32, "xw")
         nc.sync.dma_start(xw[:].bitcast(I32), x_words[0].rearrange("p n t -> p (n t)").bitcast(I32))
         wa_raw = load_weight(wa, "wa")
         wb_raw = load_weight(wb, "wb")
-        l_n1 = load_list(n1, "l_n1")
-        l_n2 = load_list(n2, "l_n2")
         w1w = sb([P, 2 * N], U8, "w1w")
         nc.sync.dma_start(w1w[:].bitcast(I32), w1_words[0].bitcast(I32))
-        w1s = load_scales(w1_scales, N, "w1s")
+        w1s = load_scales(nc.sync, w1_scales, N, "w1s")
         gate = sb([P, R], F32, "gate")
         nc.sync.dma_start(gate[:], gt.rearrange("(p t) o -> p (t o)", t=R))
         l_n3 = load_list(n3, "l_n3")
         l_n4 = load_list(n4, "l_n4")
         l_n5 = load_list(n5, "l_n5")
 
-        def pick_scales(lst, name):
-            picked = sb([P, S], U8, name + "_sg")
-            nc.vector.tensor_copy(picked[:], xs[:].indirect(lst[:]))
-            dealt = sb([P, S], U8, name + "_sd")
+        def gather(window, lst, dtype, name):
+            picked = sb([P, S], dtype, name)
+            nc.vector.tensor_copy(picked[:], window[:].indirect(lst[:]))
+            return picked
+
+        def deal(src, dtype, run, size, name):
+            dealt = sb([P, S * size], dtype, name)
             nc.vector.tensor_copy(
-                dealt[:].rearrange("p (t c i) -> p c t i", t=R, i=16),
-                picked[:].rearrange("p (c i t) -> p c t i", t=R, i=16),
+                dealt[:].rearrange("p (t c i b) -> p c t i b", t=R, i=run, b=size),
+                src[:].rearrange("p (c i t b) -> p c t i b", t=R, i=run, b=size),
             )
             return dealt
 
-        def pick_words(lst, name):
-            picked = sb([P, S], U32, name + "_g")
-            nc.vector.tensor_copy(picked[:], xw[:].indirect(lst[:]))
-            dealt = sb([P, S], U32, name + "_d")
-            nc.vector.tensor_copy(
-                dealt[:].rearrange("p (t c i) -> p c t i", t=R, i=4),
-                picked[:].rearrange("p (c i t) -> p c t i", t=R, i=4),
-            )
-            return dealt
+        def turn_add(bank, sources):
+            for n, src in enumerate(sources):
+                nc.tensor.matmul(bank, src, ident[:], start=(n == 0), stop=(n == len(sources) - 1), is_transpose=True)
 
         def project(words, word_scales, codes, scales, t):
-            acc = psum.tile([P, H], F32, name="acc")
+            acc = psum.tile([P, H], F32, name="acc", tag="wide", bufs=3)
             nc.tensor.matmul_mx(
                 acc[:],
                 lhsT=words[:, P * t : P * (t + 1)].bitcast(FP8X4),
@@ -120,22 +119,22 @@ def tile_picked_twtflowblse_none_po_kernel(tc, x_words, x_scales, wa, wb, gt, w1
             )
             return acc
 
-        xa_s = pick_scales(l_offs, "xa")
-        xb_s = pick_scales(l_two, "xb")
-        xa = pick_words(l_offs, "xa")
-        wa_codes, wa_scales = quantise_weight(wa_raw, "wa")
-        xb = pick_words(l_two, "xb")
+        ident = sb([P, P], F32, "ident")
+        make_identity(nc, ident[:])
 
-        w1w_d = sb([P, 2 * N], U8, "w1w_d")
-        nc.vector.tensor_copy(
-            w1w_d[:].rearrange("p (t c i b) -> p c t i b", t=R, i=8, b=2),
-            w1w[:].rearrange("p (c i t b) -> p c t i b", t=R, i=8, b=2),
-        )
-        w1s_d = sb([P, N], U8, "w1s_d")
-        nc.vector.tensor_copy(
-            w1s_d[:].rearrange("p (t c i) -> p c t i", t=R, i=16),
-            w1s[:].rearrange("p (c i t) -> p c t i", t=R, i=16),
-        )
+        xa_sg = gather(xs, l_offs, U8, "xa_sg")
+        xb_sg = gather(xs, l_two, U8, "xb_sg")
+        xa_s = deal(xa_sg, U8, 16, 1, "xa_s")
+        xa_g = gather(xw, l_offs, U32, "xa_g")
+        wa_codes, wa_scales = quantise_weight(wa_raw, "wa")
+        xa = deal(xa_g, U32, 4, 1, "xa")
+        xb_g = gather(xw, l_two, U32, "xb_g")
+        xb_s = deal(xb_sg, U8, 16, 1, "xb_s")
+        xb = deal(xb_g, U32, 4, 1, "xb")
+        w1w_d = deal(w1w, U8, 8, 2, "w1w_d")
+        w1s_d = deal(w1s, U8, 16, 1, "w1s_d")
+        half_gate = sb([P, R], F32, "half_gate")
+        nc.vector.tensor_scalar(half_gate[:], gate[:], 0.5, None, ALU.mult)
 
         y_win = [sb([P, H], F32, "y_win%d" % t) for t in range(R)]
         y_pl = [sb([P, H], F32, "y_pl%d" % t) for t in range(R)]
@@ -158,31 +157,58 @@ def tile_picked_twtflowblse_none_po_kernel(tc, x_words, x_scales, wa, wb, gt, w1
         d_win = [sb([P, H], F32, "d_win%d" % t) for t in range(R)]
         for t in range(R):
             acc = project(xb, xb_s, wb_codes, wb_scales, t)
-            nc.scalar.activation(d_win[t][:], acc[:], ACT.Copy, scale=gate[:, t : t + 1])
+            nc.scalar.activation(d_win[t][:], acc[:], ACT.Copy, scale=half_gate[:, t : t + 1])
 
         ex_win = [sb([P, H], F32, "ex_win%d" % t) for t in range(R)]
-        ex_pl = [sb([P, H], F32, "ex_pl%d" % t) for t in range(R)]
-        nh_win = [sb([P, H], F32, "nh_win%d" % t) for t in range(R)]
-        for k, (c0, c1) in enumerate(CHUNKS):
-            w = c1 - c0
-            term1 = sb([P, R, w], F32, "term1_%d" % k)
-            term2 = sb([P, R, w], F32, "term2_%d" % k)
-            z = sb([P, R, w], F32, "z%d" % k)
+        h_win = [sb([P, H], F32, "h_win%d" % t) for t in range(R)]
+        flat = "p t c -> p (t c)"
+
+        def terms(k):
+            c0, c1 = CHUNKS[k]
+            term1 = sb([P, R, c1 - c0], F32, "term1_%d" % k)
+            term2 = sb([P, R, c1 - c0], F32, "term2_%d" % k)
             for t in range(R):
-                nc.vector.tensor_tensor(term1[:, t, :], diff1[t][:, c0:c1], d_win[t][:, c0:c1], ALU.mult)
+                nc.vector.scalar_tensor_tensor(term1[:, t, :], diff1[t][:, c0:c1], 2.0, d_win[t][:, c0:c1], ALU.mult, ALU.mult)
             for t in range(R):
                 nc.vector.tensor_tensor(term2[:, t, :], d_win[t][:].indirect(entries(l_n3, c0, c1)), diff2[t][:, c0:c1], ALU.mult)
-            flat = "p t c -> p (t c)"
-            nc.vector.scalar_tensor_tensor(z[:].rearrange(flat), term2[:].rearrange(flat), 0.5, term1[:].rearrange(flat), ALU.mult, ALU.add)
-            z_bf = sb([P, R * w], BF16, "z_bf%d" % k)
-            interleave(nc.vector.tensor_copy if k == len(CHUNKS) - 1 else nc.scalar.copy, z_bf[:], z[:])
+            return term1, term2
+
+        def sum_on_tensor(k, term1, term2):
+            c0, c1 = CHUNKS[k]
+            z_bf = sb([P, R * (c1 - c0)], BF16, "z_bf%d" % k)
+            for b0 in range(0, c1 - c0, P):
+                z_turned = psum.tile([P, R, P], F32, name="z_turned", tag="turn", bufs=2)
+                for t in range(R):
+                    turn_add(z_turned[:, t, :], (term1[:, t, b0 : b0 + P], term2[:, t, b0 : b0 + P]))
+                pairs = keep.tile([P, R * P], BF16, name="pairs", bufs=2, align_bytes=64)
+                nc.scalar.copy(pairs[:].rearrange("j (u p e) -> j u p e", u=2, e=2), z_turned[:].rearrange("j (u e) p -> j u p e", u=2))
+                back = psum.tile([P, 2, P], F32, name="back", tag="back", bufs=1)
+                for u in range(2):
+                    nc.tensor.transpose(back[:, u, :], pairs[:].bitcast(F32)[:, P * u : P * (u + 1)], ident[:])
+                words = z_bf[:, R * b0 : R * (b0 + P)].bitcast(F32)
+                nc.scalar.copy(words.rearrange("p (j u) -> p j u", u=2), back[:].rearrange("p u j -> p j u"))
+            return z_bf
+
+        def sum_on_vector(k, term1, term2):
+            c0, c1 = CHUNKS[k]
+            z = sb([P, R, c1 - c0], F32, "z%d" % k)
+            nc.vector.tensor_tensor(z[:].rearrange(flat), term1[:].rearrange(flat), term2[:].rearrange(flat), ALU.add)
+            return z
+
+        def mix(k, z_bf):
+            c0, c1 = CHUNKS[k]
+            w = c1 - c0
             z_codes = sb([P, w], U32, "z_codes%d" % k)
             z_scales = sb([P, w], U8, "z_scales%d" % k)
             nc.vector.quantize_mx(z_codes[:].bitcast(FP8X4), z_scales[:], z_bf[:])
+            per_bank = H // w
+            banks = []
             for t in range(R):
-                hacc = psum.tile([P, H], F32, name="hacc")
+                if t % per_bank == 0:
+                    hacc = psum.tile([P, per_bank, w], F32, name="hacc", tag="hacc", bufs=2)
+                banks.append(hacc[:, t % per_bank, :])
                 nc.tensor.matmul_mx(
-                    hacc[:, 0:w],
+                    banks[t],
                     lhsT=w1w_d[:, 2 * P * t : 2 * P * (t + 1)].bitcast(FP4X4),
                     lhsT_scale=w1s_d[:, P * t : P * (t + 1)],
                     rhs=z_codes[:].bitcast(FP8X4),
@@ -190,34 +216,62 @@ def tile_picked_twtflowblse_none_po_kernel(tc, x_words, x_scales, wa, wb, gt, w1
                     start=True,
                     stop=True,
                 )
-                nc.scalar.activation(ex_win[t][:, c0:c1], hacc[:, 0:w], ACT.Exp)
-                nc.scalar.activation(ex_pl[t][:, c0:c1], hacc[:, 0:w], ACT.Exp)
-                nc.scalar.activation(nh_win[t][:, c0:c1], hacc[:, 0:w], ACT.Copy, scale=-1.0)
-
-        logs = []
-        for u, (c0, c1) in enumerate(HALVES):
-            both = sb([P, R, HALF], F32, "both%d" % u)
             for t in range(R):
-                nc.vector.tensor_tensor(both[:, t, :], ex_win[t][:].indirect(entries(l_n4, c0, c1)), ex_pl[t][:, c0:c1], ALU.add)
-            lg = sb([P, R, HALF], F32, "lg%d" % u)
-            nc.scalar.activation(lg[:], both[:], ACT.Ln)
-            logs.append(lg)
+                te = (t + 1) % R
+                nc.scalar.activation(ex_win[te][:, c0:c1], banks[te], ACT.Exp)
+                nc.scalar.copy(h_win[t][:, c0:c1], banks[t])
+
+        z_bf0 = sum_on_tensor(0, *terms(0))
+        z_bf1 = sum_on_tensor(1, *terms(1))
+        mix(0, z_bf0)
+        z_last = sum_on_vector(2, *terms(2))
+        mix(1, z_bf1)
+        z_bf2 = sb([P, R * P], BF16, "z_bf2")
+        interleave(nc.vector.tensor_copy, z_bf2[:], z_last[:])
+        mix(2, z_bf2)
+
+        ex4 = [sb([P, H], F32, "ex4_%d" % t) for t in range(R)]
+        units = [(t, half) for t in range(R) for half in HALVES]
+        for t, (c0, c1) in units[:SCALAR_UNITS]:
+            nc.scalar.activation(ex4[t][:, c0:c1], h_win[t][:].indirect(entries(l_n4, c0, c1)), ACT.Exp)
+        for t, (c0, c1) in units[SCALAR_UNITS:]:
+            nc.vector.tensor_copy(ex4[t][:, c0:c1], ex_win[t][:].indirect(entries(l_n4, c0, c1)))
+        h5 = [sb([P, R, HALF], F32, "h5_%d" % u) for u in range(2)]
+        for u, (c0, c1) in enumerate(HALVES):
+            for t in range(R):
+                nc.vector.tensor_copy(h5[u][:, t, :], h_win[t][:].indirect(entries(l_n5, c0, c1)))
 
         o_scales = sb([P, H], U8, "o_scales")
         out_rows = out_0.rearrange("(p t) c -> p t c", t=R)
         out_words = out_1[0].rearrange("p c t -> p (c t)").bitcast(I32)
-        for k, (c0, c1) in enumerate(CHUNKS):
-            w = c1 - c0
-            lg = logs[c0 // HALF]
-            o = sb([P, R, w], F32, "o%d" % k)
+        blocks = H // P
+        logs = []
+        for b in range(blocks):
+            cols = slice(P * b, P * (b + 1))
+            both = psum.tile([P, R, P], F32, name="both", tag="wide", bufs=3)
             for t in range(R):
-                nc.vector.tensor_tensor(o[:, t, :], nh_win[t][:].indirect(entries(l_n5, c0, c1)), lg[:, t, c0 % HALF : c0 % HALF + w], ALU.add)
-            nc.sync.dma_start(out_rows[:, :, c0:c1], o[:])
-            o_bf = sb([P, R * w], BF16, "o_bf%d" % k)
-            interleave(nc.vector.tensor_copy if k == len(CHUNKS) - 1 else nc.scalar.copy, o_bf[:], o[:])
-            o_codes = sb([P, w], U32, "o_codes%d" % k)
-            nc.vector.quantize_mx(o_codes[:].bitcast(FP8X4), o_scales[:, c0:c1], o_bf[:])
-            nc.sync.dma_start(out_words[:, c0:c1], o_codes[:].bitcast(I32))
+                turn_add(both[:, t, :], (ex_win[t][:, cols], ex4[t][:, cols]))
+            lg = sb([P, R, P], F32, "lg%d" % b)
+            nc.scalar.activation(lg[:], both[:], ACT.Ln)
+            logs.append(lg)
+        rounded = []
+        for b in range(blocks):
+            lg_back = psum.tile([P, R, P], F32, name="lg_back", tag="turn", bufs=2)
+            for t in range(R):
+                nc.tensor.transpose(lg_back[:, t, :], logs[b][:, t, :], ident[:])
+            o = sb([P, R, P], F32, "o%d" % b)
+            h0 = (P * b) % HALF
+            nc.vector.tensor_tensor(o[:], lg_back[:], h5[P * b // HALF][:, :, h0 : h0 + P], ALU.subtract)
+            nc.sync.dma_start(out_rows[:, :, P * b : P * (b + 1)], o[:])
+            o_bf = sb([P, R * P], BF16, "o_bf%d" % b)
+            interleave(nc.vector.tensor_copy if b == blocks - 1 else nc.scalar.copy, o_bf[:], o[:])
+            rounded.append(o_bf)
+        o_codes = sb([P, H], U32, "o_codes")
+        for b in range(blocks):
+            cols = slice(P * b, P * (b + 1))
+            nc.vector.quantize_mx(o_codes[:, cols].bitcast(FP8X4), o_scales[:, cols], rounded[b][:])
+        for c0, c1 in ((0, H - P), (H - P, H)):
+            nc.sync.dma_start(out_words[:, c0:c1], o_codes[:, c0:c1].bitcast(I32))
         for q in range(4):
             queue = nc.scalar if q % 2 else nc.sync
             queue.dma_start(out_2[0, 4 * q : 4 * q + 4, :].bitcast(I32), o_scales[32 * q : 32 * q + 4, :].bitcast(I32))

@@ -22,7 +22,6 @@ R = 4
 HALF = 256
 HALVES = ((0, 256), (256, 512))
 CHUNKS = ((0, 256), (256, 384), (384, 512))
-SCALAR_UNITS = 3
 
 
 def tile_picked_twtflowblse_none_po_kernel(tc, x_words, x_scales, wa, wb, gt, w1_words, w1_scales, offs, two, n1, n2, n3, n4, n5, out_0, out_1, out_2):
@@ -38,14 +37,14 @@ def tile_picked_twtflowblse_none_po_kernel(tc, x_words, x_scales, wa, wb, gt, w1
             nc.sync.dma_start(tile[:], src)
             return tile
 
-        def sb(shape, dtype, name):
-            return keep.tile(shape, dtype, name=name, align_bytes=64)
+        def sb(shape, dtype, name, tag=""):
+            return keep.tile(shape, dtype, name=name, tag=tag, align_bytes=64)
 
         def entries(lst, c0, c1):
             return lst[:, c0 // 16 : c1 // 16]
 
         def load_scales(queue, src, width, name):
-            plane = sb([P, width], U8, name)
+            plane = sb([P, width], U8, name, name)
             nc.vector.memset(plane[:].bitcast(I32), 0)
             for q in range(4):
                 queue.dma_start(plane[32 * q : 32 * q + 4, :].bitcast(I32), src[0, 4 * q : 4 * q + 4, :].bitcast(I32))
@@ -89,8 +88,8 @@ def tile_picked_twtflowblse_none_po_kernel(tc, x_words, x_scales, wa, wb, gt, w1
         l_n4 = load_list(n4, "l_n4")
         l_n5 = load_list(n5, "l_n5")
 
-        def gather(window, lst, dtype, name):
-            picked = sb([P, S], dtype, name)
+        def gather(window, lst, dtype, name, tag=""):
+            picked = sb([P, S], dtype, name, tag)
             nc.vector.tensor_copy(picked[:], window[:].indirect(lst[:]))
             return picked
 
@@ -107,7 +106,7 @@ def tile_picked_twtflowblse_none_po_kernel(tc, x_words, x_scales, wa, wb, gt, w1
                 nc.tensor.matmul(bank, src, ident[:], start=(n == 0), stop=(n == len(sources) - 1), is_transpose=True)
 
         def project(words, word_scales, codes, scales, t):
-            acc = psum.tile([P, H], F32, name="acc", tag="wide", bufs=3)
+            acc = psum.tile([P, H], F32, name="acc", tag="wide", bufs=4)
             nc.tensor.matmul_mx(
                 acc[:],
                 lhsT=words[:, P * t : P * (t + 1)].bitcast(FP8X4),
@@ -125,64 +124,67 @@ def tile_picked_twtflowblse_none_po_kernel(tc, x_words, x_scales, wa, wb, gt, w1
         xa_sg = gather(xs, l_offs, U8, "xa_sg")
         xb_sg = gather(xs, l_two, U8, "xb_sg")
         xa_s = deal(xa_sg, U8, 16, 1, "xa_s")
-        xa_g = gather(xw, l_offs, U32, "xa_g")
+        xa_g = gather(xw, l_offs, U32, "xa_g", "xs")
         wa_codes, wa_scales = quantise_weight(wa_raw, "wa")
         xa = deal(xa_g, U32, 4, 1, "xa")
-        xb_g = gather(xw, l_two, U32, "xb_g")
+        xb_g = gather(xw, l_two, U32, "xb_g", "xs")
         xb_s = deal(xb_sg, U8, 16, 1, "xb_s")
         xb = deal(xb_g, U32, 4, 1, "xb")
         w1w_d = deal(w1w, U8, 8, 2, "w1w_d")
         w1s_d = deal(w1s, U8, 16, 1, "w1s_d")
         half_gate = sb([P, R], F32, "half_gate")
-        nc.vector.tensor_scalar(half_gate[:], gate[:], 0.5, None, ALU.mult)
+        nc.scalar.activation(half_gate[:], gate[:], ACT.Copy, scale=0.5)
 
         y_win = [sb([P, H], F32, "y_win%d" % t) for t in range(R)]
-        y_pl = [sb([P, H], F32, "y_pl%d" % t) for t in range(R)]
-        diff1 = [sb([P, H], F32, "diff1_%d" % t) for t in range(R)]
-        diff2 = [sb([P, H], F32, "diff2_%d" % t) for t in range(R)]
+        ex_win = [sb([P, 2 * H], F32, "ex_win%d" % t) for t in range(R)]
+        ex_last = sb([P, H], F32, "ex_last")
+        y_rest = sb([P, R - 1, H], F32, "y_rest")
+        y_pl = [ex_win[0][:, H:]] + [y_rest[:, t, :] for t in range(R - 1)]
+        ex_pl = [ex_win[t + 1][:, H:] for t in range(R - 1)] + [ex_last[:]]
         for t in range(R):
             acc = project(xa, xa_s, wa_codes, wa_scales, t)
             nc.scalar.copy(y_win[t][:], acc[:])
-            nc.scalar.copy(y_pl[t][:], acc[:])
+            nc.scalar.copy(y_pl[t], acc[:])
 
-        def differences(c0, c1):
-            for t in range(R):
-                nc.vector.tensor_tensor(diff1[t][:, c0:c1], y_win[t][:].indirect(entries(l_n1, c0, c1)), y_pl[t][:, c0:c1], ALU.subtract)
-                nc.vector.tensor_tensor(diff2[t][:, c0:c1], y_win[t][:].indirect(entries(l_n2, c0, c1)), y_pl[t][:, c0:c1], ALU.subtract)
-
-        differences(*HALVES[0])
         wb_codes, wb_scales = quantise_weight(wb_raw, "wb")
-        differences(*HALVES[1])
+
+        def difference(t, lst, u, tag):
+            c0, c1 = HALVES[u]
+            diff = sb([P, HALF], F32, "%s_%d" % (tag, u), tag)
+            nc.vector.tensor_tensor(diff[:], y_win[t][:].indirect(entries(lst, c0, c1)), y_pl[t][:, c0:c1], ALU.subtract)
+            return diff
 
         d_win = [sb([P, H], F32, "d_win%d" % t) for t in range(R)]
         for t in range(R):
             acc = project(xb, xb_s, wb_codes, wb_scales, t)
             nc.scalar.activation(d_win[t][:], acc[:], ACT.Copy, scale=half_gate[:, t : t + 1])
 
-        ex_win = [sb([P, H], F32, "ex_win%d" % t) for t in range(R)]
-        h_win = [sb([P, H], F32, "h_win%d" % t) for t in range(R)]
+        nh_win = [sb([P, H], F32, "nh_win%d" % t) for t in range(R)]
         flat = "p t c -> p (t c)"
 
-        def terms(k):
+        def terms(k, diff1, diff2):
             c0, c1 = CHUNKS[k]
+            part = slice(c0 % HALF, c0 % HALF + c1 - c0)
             term1 = sb([P, R, c1 - c0], F32, "term1_%d" % k)
             term2 = sb([P, R, c1 - c0], F32, "term2_%d" % k)
             for t in range(R):
-                nc.vector.scalar_tensor_tensor(term1[:, t, :], diff1[t][:, c0:c1], 2.0, d_win[t][:, c0:c1], ALU.mult, ALU.mult)
+                nc.vector.scalar_tensor_tensor(term1[:, t, :], diff1[t][:, part], 2.0, d_win[t][:, c0:c1], ALU.mult, ALU.mult)
             for t in range(R):
-                nc.vector.tensor_tensor(term2[:, t, :], d_win[t][:].indirect(entries(l_n3, c0, c1)), diff2[t][:, c0:c1], ALU.mult)
+                nc.vector.tensor_tensor(term2[:, t, :], d_win[t][:].indirect(entries(l_n3, c0, c1)), diff2[t][:, part], ALU.mult)
             return term1, term2
 
         def sum_on_tensor(k, term1, term2):
             c0, c1 = CHUNKS[k]
-            z_bf = sb([P, R * (c1 - c0)], BF16, "z_bf%d" % k)
-            for b0 in range(0, c1 - c0, P):
-                z_turned = psum.tile([P, R, P], F32, name="z_turned", tag="turn", bufs=2)
-                for t in range(R):
+            z_bf = sb([P, R * (c1 - c0)], BF16, "z_bf%d" % k, "z_slot%d" % k)
+            starts = range(0, c1 - c0, P)
+            banks = [psum.tile([P, R, P], F32, name="z_turned", tag="turn", bufs=2) for b0 in starts]
+            for t in range(R):
+                for b0, z_turned in zip(starts, banks):
                     turn_add(z_turned[:, t, :], (term1[:, t, b0 : b0 + P], term2[:, t, b0 : b0 + P]))
+            for b0, z_turned in zip(starts, banks):
                 pairs = keep.tile([P, R * P], BF16, name="pairs", bufs=2, align_bytes=64)
                 nc.scalar.copy(pairs[:].rearrange("j (u p e) -> j u p e", u=2, e=2), z_turned[:].rearrange("j (u e) p -> j u p e", u=2))
-                back = psum.tile([P, 2, P], F32, name="back", tag="back", bufs=1)
+                back = psum.tile([P, 2, P], F32, name="back", tag="back", bufs=2)
                 for u in range(2):
                     nc.tensor.transpose(back[:, u, :], pairs[:].bitcast(F32)[:, P * u : P * (u + 1)], ident[:])
                 words = z_bf[:, R * b0 : R * (b0 + P)].bitcast(F32)
@@ -201,14 +203,9 @@ def tile_picked_twtflowblse_none_po_kernel(tc, x_words, x_scales, wa, wb, gt, w1
             z_codes = sb([P, w], U32, "z_codes%d" % k)
             z_scales = sb([P, w], U8, "z_scales%d" % k)
             nc.vector.quantize_mx(z_codes[:].bitcast(FP8X4), z_scales[:], z_bf[:])
-            per_bank = H // w
-            banks = []
             for t in range(R):
-                if t % per_bank == 0:
-                    hacc = psum.tile([P, per_bank, w], F32, name="hacc", tag="hacc", bufs=2)
-                banks.append(hacc[:, t % per_bank, :])
                 nc.tensor.matmul_mx(
-                    banks[t],
+                    h_bank[t][:, c0:c1],
                     lhsT=w1w_d[:, 2 * P * t : 2 * P * (t + 1)].bitcast(FP4X4),
                     lhsT_scale=w1s_d[:, P * t : P * (t + 1)],
                     rhs=z_codes[:].bitcast(FP8X4),
@@ -216,62 +213,75 @@ def tile_picked_twtflowblse_none_po_kernel(tc, x_words, x_scales, wa, wb, gt, w1
                     start=True,
                     stop=True,
                 )
-            for t in range(R):
-                te = (t + 1) % R
-                nc.scalar.activation(ex_win[te][:, c0:c1], banks[te], ACT.Exp)
-                nc.scalar.copy(h_win[t][:, c0:c1], banks[t])
+                nc.scalar.activation(ex_win[t][:, c0:c1], h_bank[t][:, c0:c1], ACT.Exp)
+                if k == 0:
+                    nc.sync.dma_start(ex_pl[t][:, c0:c1], ex_win[t][:, c0:c1])
+                else:
+                    nc.scalar.activation(ex_pl[t][:, c0:c1], h_bank[t][:, c0:c1], ACT.Exp)
 
-        z_bf0 = sum_on_tensor(0, *terms(0))
-        z_bf1 = sum_on_tensor(1, *terms(1))
+        h_bank = [psum.tile([P, H], F32, name="h_bank%d" % t, tag="wide", bufs=4) for t in range(R)]
+        diff1, diff2 = [], []
+        for t in range(R):
+            diff1.append(difference(t, l_n1, 0, "diff1_%d" % t))
+            diff2.append(difference(t, l_n2, 0, "diff2_%d" % t))
+        z_bf0 = sum_on_tensor(0, *terms(0, diff1, diff2))
         mix(0, z_bf0)
-        z_last = sum_on_vector(2, *terms(2))
+        diff1, diff2 = [], []
+        for t in range(R):
+            diff1.append(difference(t, l_n1, 1, "diff1_%d" % t))
+            diff2.append(difference(t, l_n2, 1, "diff2_%d" % t if t < R - 1 else "z_slot0"))
+        mid_terms = terms(1, diff1, diff2)
+        z_bf1 = sum_on_tensor(1, *mid_terms)
+        last_terms = terms(2, diff1, diff2)
+        z_last = sum_on_vector(2, *last_terms)
         mix(1, z_bf1)
-        z_bf2 = sb([P, R * P], BF16, "z_bf2")
+        z_bf2 = sb([P, R * P], BF16, "z_bf2", "z_slot1")
         interleave(nc.vector.tensor_copy, z_bf2[:], z_last[:])
         mix(2, z_bf2)
 
-        ex4 = [sb([P, H], F32, "ex4_%d" % t) for t in range(R)]
-        units = [(t, half) for t in range(R) for half in HALVES]
-        for t, (c0, c1) in units[:SCALAR_UNITS]:
-            nc.scalar.activation(ex4[t][:, c0:c1], h_win[t][:].indirect(entries(l_n4, c0, c1)), ACT.Exp)
-        for t, (c0, c1) in units[SCALAR_UNITS:]:
-            nc.vector.tensor_copy(ex4[t][:, c0:c1], ex_win[t][:].indirect(entries(l_n4, c0, c1)))
-        h5 = [sb([P, R, HALF], F32, "h5_%d" % u) for u in range(2)]
-        for u, (c0, c1) in enumerate(HALVES):
-            for t in range(R):
-                nc.vector.tensor_copy(h5[u][:, t, :], h_win[t][:].indirect(entries(l_n5, c0, c1)))
+        sums, logs = [], []
+        for t in range(R):
+            nc.scalar.activation(nh_win[t][:], h_bank[t][:], ACT.Copy, scale=-1.0)
+            both = sb([P, H], F32, "both%d" % t)
+            nc.vector.tensor_tensor(both[:], ex_win[t][:].indirect(l_n4[:]), ex_pl[t], ALU.add)
+            lg = sb([P, H], F32, "lg%d" % t)
+            nc.scalar.activation(lg[:, 0:HALF], both[:, 0:HALF], ACT.Ln)
+            sums.append(both)
+            logs.append(lg)
+        for t in range(R):
+            nc.scalar.activation(logs[t][:, HALF:], sums[t][:, HALF:], ACT.Ln)
 
         o_scales = sb([P, H], U8, "o_scales")
+        o_codes = sb([P, H], U32, "o_codes")
         out_rows = out_0.rearrange("(p t) c -> p t c", t=R)
         out_words = out_1[0].rearrange("p c t -> p (c t)").bitcast(I32)
-        blocks = H // P
-        logs = []
-        for b in range(blocks):
-            cols = slice(P * b, P * (b + 1))
-            both = psum.tile([P, R, P], F32, name="both", tag="wide", bufs=3)
+
+        def finish(k):
+            c0, c1 = CHUNKS[k]
+            o = sb([P, R, c1 - c0], F32, "o%d" % k)
             for t in range(R):
-                turn_add(both[:, t, :], (ex_win[t][:, cols], ex4[t][:, cols]))
-            lg = sb([P, R, P], F32, "lg%d" % b)
-            nc.scalar.activation(lg[:], both[:], ACT.Ln)
-            logs.append(lg)
-        rounded = []
-        for b in range(blocks):
-            lg_back = psum.tile([P, R, P], F32, name="lg_back", tag="turn", bufs=2)
-            for t in range(R):
-                nc.tensor.transpose(lg_back[:, t, :], logs[b][:, t, :], ident[:])
-            o = sb([P, R, P], F32, "o%d" % b)
-            h0 = (P * b) % HALF
-            nc.vector.tensor_tensor(o[:], lg_back[:], h5[P * b // HALF][:, :, h0 : h0 + P], ALU.subtract)
-            nc.sync.dma_start(out_rows[:, :, P * b : P * (b + 1)], o[:])
-            o_bf = sb([P, R * P], BF16, "o_bf%d" % b)
-            interleave(nc.vector.tensor_copy if b == blocks - 1 else nc.scalar.copy, o_bf[:], o[:])
-            rounded.append(o_bf)
-        o_codes = sb([P, H], U32, "o_codes")
-        for b in range(blocks):
-            cols = slice(P * b, P * (b + 1))
-            nc.vector.quantize_mx(o_codes[:, cols].bitcast(FP8X4), o_scales[:, cols], rounded[b][:])
-        for c0, c1 in ((0, H - P), (H - P, H)):
+                nc.vector.tensor_tensor(o[:, t, :], nh_win[t][:].indirect(entries(l_n5, c0, c1)), logs[t][:, c0:c1], ALU.add)
+            nc.sync.dma_start(out_rows[:, :, c0:c1], o[:])
+            return o
+
+        def round_out(k, o, engine_copy):
+            c0, c1 = CHUNKS[k]
+            o_bf = sb([P, R * (c1 - c0)], BF16, "o_bf%d" % k)
+            interleave(engine_copy, o_bf[:], o[:])
+            return o_bf
+
+        def planes(k, o_bf):
+            c0, c1 = CHUNKS[k]
+            nc.vector.quantize_mx(o_codes[:, c0:c1].bitcast(FP8X4), o_scales[:, c0:c1], o_bf[:])
             nc.sync.dma_start(out_words[:, c0:c1], o_codes[:, c0:c1].bitcast(I32))
+
+        o_bf0 = round_out(0, finish(0), nc.scalar.copy)
+        o_bf1 = round_out(1, finish(1), nc.scalar.copy)
+        o_last = finish(2)
+        planes(0, o_bf0)
+        o_bf2 = round_out(2, o_last, nc.vector.tensor_copy)
+        planes(1, o_bf1)
+        planes(2, o_bf2)
         for q in range(4):
             queue = nc.scalar if q % 2 else nc.sync
             queue.dma_start(out_2[0, 4 * q : 4 * q + 4, :].bitcast(I32), o_scales[32 * q : 32 * q + 4, :].bitcast(I32))

@@ -3,7 +3,7 @@ from contextlib import ExitStack
 import concourse.mybir as mybir
 from concourse.masks import make_identity
 
-K, T, S, N, H = 512, 2048, 512, 512, 512
+T, S, N, H = 2048, 512, 512, 512
 FLOPS = 3 * 2 * 512 * 512 * 512
 
 F32 = mybir.dt.float32
@@ -19,12 +19,17 @@ ACT = mybir.ActivationFunctionType
 
 P = 128
 R = 4
-HALF = 256
-HALVES = ((0, 256), (256, 512))
-CHUNKS = ((0, 256), (256, 384), (384, 512))
+QUADRANTS = 4
+PER_COLUMN = 16
+LINE = 16
+HALF = H // 2
+HALVES = ((0, HALF), (HALF, H))
+CHUNKS = ((0, HALF), (HALF, H - P), (H - P, H))
 
 
-def tile_picked_twtflowblse_none_po_kernel(tc, x_words, x_scales, wa, wb, gt, w1_words, w1_scales, offs, two, n1, n2, n3, n4, n5, out_0, out_1, out_2):
+def tile_picked_twtflowblse_none_po_kernel(
+    tc, x_words, x_scales, wa, wb, gt, w1_words, w1_scales, offs, two, n1, n2, n3, n4, n5, out_0, out_1, out_2
+):
     nc = tc.nc
 
     with ExitStack() as ctx:
@@ -32,81 +37,79 @@ def tile_picked_twtflowblse_none_po_kernel(tc, x_words, x_scales, wa, wb, gt, w1
         keep = ctx.enter_context(tc.tile_pool(name="keep", bufs=1))
         psum = ctx.enter_context(tc.psum_pool(name="psum", bufs=1))
 
-        def load_list(src, name):
-            tile = lists.tile([P, 32], U16, name=name)
-            nc.sync.dma_start(tile[:], src)
-            return tile
-
         def sb(shape, dtype, name, tag=""):
             return keep.tile(shape, dtype, name=name, tag=tag, align_bytes=64)
 
+        def load_list(src, name):
+            tile = lists.tile([P, S // PER_COLUMN], U16, name=name)
+            nc.sync.dma_start(tile[:], src)
+            return tile
+
         def entries(lst, c0, c1):
-            return lst[:, c0 // 16 : c1 // 16]
+            return lst[:, c0 // PER_COLUMN : c1 // PER_COLUMN]
 
-        def load_scales(queue, src, width, name):
-            plane = sb([P, width], U8, name, name)
-            nc.vector.memset(plane[:].bitcast(I32), 0)
-            for q in range(4):
-                queue.dma_start(plane[32 * q : 32 * q + 4, :].bitcast(I32), src[0, 4 * q : 4 * q + 4, :].bitcast(I32))
-            return plane
+        def load_scales(queues, src, width, name):
+            tile = sb([P, width], U8, name)
+            nc.vector.memset(tile[:].bitcast(I32), 0)
+            for q in range(QUADRANTS):
+                queues[q % 2].dma_start(tile[32 * q : 32 * q + 4, :].bitcast(I32), src[0, 4 * q : 4 * q + 4, :].bitcast(I32))
+            return tile
 
-        def load_weight(w, name):
-            halves = []
-            for u, (c0, c1) in enumerate(HALVES):
-                raw = sb([P, R, HALF], F32, "%s_raw%d" % (name, u))
-                nc.sync.dma_start(raw[:], w.rearrange("(p t) c -> p t c", t=R)[:, :, c0:c1])
-                halves.append(raw)
-            return halves
+        def load_weight(weight, name):
+            raw = sb([P, R, H], F32, name + "_raw")
+            nc.sync.dma_start(raw[:], weight.rearrange("(p t) c -> p t c", t=R))
+            return raw
 
-        def interleave(engine_copy, dst, src):
-            engine_copy(dst.rearrange("p (c i t) -> p c t i", i=4, t=R), src.rearrange("p t (c i) -> p c t i", i=4))
+        def round_rows(engine_copy, dst, src):
+            run = LINE // 4
+            engine_copy(dst.rearrange("p (c i t) -> p c t i", i=run, t=R), src.rearrange("p t (c i) -> p c t i", i=run))
 
-        def quantise_weight(halves, name):
-            grouped = sb([P, R * H], BF16, name + "_bf")
+        def round_weight(raw, name):
+            rounded = sb([P, R * H], BF16, name + "_bf")
+            for engine_copy, (c0, c1) in zip((nc.scalar.copy, nc.vector.tensor_copy), HALVES):
+                round_rows(engine_copy, rounded[:, R * c0 : R * c1], raw[:, :, c0:c1])
+            return rounded
+
+        def quantise_weight(rounded, name, tag=""):
             codes = sb([P, H], U32, name + "_codes")
-            scales = sb([P, H], U8, name + "_scales")
-            for raw, (c0, c1) in zip(halves, HALVES):
-                interleave(nc.scalar.copy, grouped[:, R * c0 : R * c1], raw[:])
-            nc.vector.quantize_mx(codes[:].bitcast(FP8X4), scales[:], grouped[:])
+            scales = sb([P, H], U8, name + "_scales", tag)
+            nc.vector.quantize_mx(codes[:].bitcast(FP8X4), scales[:], rounded[:])
             return codes, scales
 
-        xs = load_scales(nc.scalar, x_scales, T, "xs")
+        x_scale_table = load_scales((nc.scalar, nc.sync), x_scales, T, "x_scale_table")
         l_offs = load_list(offs, "l_offs")
         l_two = load_list(two, "l_two")
+        w1_word_raw = sb([P, 2 * N], U8, "w1_word_raw")
+        nc.sync.dma_start(w1_word_raw[:].bitcast(I32), w1_words[0].bitcast(I32))
         l_n1 = load_list(n1, "l_n1")
-        l_n2 = load_list(n2, "l_n2")
-        xw = sb([P, T], U32, "xw")
-        nc.sync.dma_start(xw[:].bitcast(I32), x_words[0].rearrange("p n t -> p (n t)").bitcast(I32))
         wa_raw = load_weight(wa, "wa")
+        x_word_table = sb([P, T], U32, "x_word_table")
+        nc.sync.dma_start(x_word_table[:].bitcast(I32), x_words[0].rearrange("p n t -> p (n t)").bitcast(I32))
+        l_n2 = load_list(n2, "l_n2")
         wb_raw = load_weight(wb, "wb")
-        w1w = sb([P, 2 * N], U8, "w1w")
-        nc.sync.dma_start(w1w[:].bitcast(I32), w1_words[0].bitcast(I32))
-        w1s = load_scales(nc.sync, w1_scales, N, "w1s")
         gate = sb([P, R], F32, "gate")
         nc.sync.dma_start(gate[:], gt.rearrange("(p t) o -> p (t o)", t=R))
         l_n3 = load_list(n3, "l_n3")
+        w1_scale_raw = load_scales((nc.sync, nc.sync), w1_scales, N, "w1_scale_raw")
         l_n4 = load_list(n4, "l_n4")
         l_n5 = load_list(n5, "l_n5")
 
-        def gather(window, lst, dtype, name, tag=""):
+        def pick(table, lst, dtype, name, tag=""):
             picked = sb([P, S], dtype, name, tag)
-            nc.vector.tensor_copy(picked[:], window[:].indirect(lst[:]))
+            nc.vector.tensor_copy(picked[:], table[:].indirect(lst[:]))
             return picked
 
-        def deal(src, dtype, run, size, name):
-            dealt = sb([P, S * size], dtype, name)
+        def deal(src, dtype, column_bytes, column_elements, name, tag=""):
+            run = LINE // column_bytes
+            dealt = sb([P, S * column_elements], dtype, name, tag)
             nc.vector.tensor_copy(
-                dealt[:].rearrange("p (t c i b) -> p c t i b", t=R, i=run, b=size),
-                src[:].rearrange("p (c i t b) -> p c t i b", t=R, i=run, b=size),
+                dealt[:].rearrange("p (t c i b) -> p c t i b", t=R, i=run, b=column_elements),
+                src[:].rearrange("p (c i t b) -> p c t i b", t=R, i=run, b=column_elements),
             )
             return dealt
 
-        def turn_add(bank, sources):
-            for n, src in enumerate(sources):
-                nc.tensor.matmul(bank, src, ident[:], start=(n == 0), stop=(n == len(sources) - 1), is_transpose=True)
-
         def project(words, word_scales, codes, scales, t):
-            acc = psum.tile([P, H], F32, name="acc", tag="wide", bufs=4)
+            acc = psum.tile([P, H], F32, name="acc", tag="wide", bufs=R)
             nc.tensor.matmul_mx(
                 acc[:],
                 lhsT=words[:, P * t : P * (t + 1)].bitcast(FP8X4),
@@ -121,56 +124,64 @@ def tile_picked_twtflowblse_none_po_kernel(tc, x_words, x_scales, wa, wb, gt, w1
         ident = sb([P, P], F32, "ident")
         make_identity(nc, ident[:])
 
-        xa_sg = gather(xs, l_offs, U8, "xa_sg")
-        xb_sg = gather(xs, l_two, U8, "xb_sg")
-        xa_s = deal(xa_sg, U8, 16, 1, "xa_s")
-        xa_g = gather(xw, l_offs, U32, "xa_g", "xs")
-        wa_codes, wa_scales = quantise_weight(wa_raw, "wa")
-        xa = deal(xa_g, U32, 4, 1, "xa")
-        xb_g = gather(xw, l_two, U32, "xb_g", "xs")
-        xb_s = deal(xb_sg, U8, 16, 1, "xb_s")
-        xb = deal(xb_g, U32, 4, 1, "xb")
-        w1w_d = deal(w1w, U8, 8, 2, "w1w_d")
-        w1s_d = deal(w1s, U8, 16, 1, "w1s_d")
+        xa_scale_picked = pick(x_scale_table, l_offs, U8, "xa_scale_picked")
+        xb_scale_picked = pick(x_scale_table, l_two, U8, "xb_scale_picked")
+        xa_scales = deal(xa_scale_picked, U8, 1, 1, "xa_scales")
+        xb_scales = deal(xb_scale_picked, U8, 1, 1, "xb_scales")
+        w1_codes = deal(w1_word_raw, U8, 2, 2, "w1_codes")
+        wa_codes, wa_scales = quantise_weight(round_weight(wa_raw, "wa"), "wa")
+        xa_codes = deal(pick(x_word_table, l_offs, U32, "xa_word_picked", "picked"), U32, 4, 1, "xa_codes")
+        xb_codes = deal(pick(x_word_table, l_two, U32, "xb_word_picked", "picked"), U32, 4, 1, "xb_codes")
         half_gate = sb([P, R], F32, "half_gate")
-        nc.scalar.activation(half_gate[:], gate[:], ACT.Copy, scale=0.5)
+        nc.gpsimd.tensor_scalar(half_gate[:], gate[:], 0.5, 0.0, ALU.mult, ALU.add)
 
         y_win = [sb([P, H], F32, "y_win%d" % t) for t in range(R)]
         ex_win = [sb([P, 2 * H], F32, "ex_win%d" % t) for t in range(R)]
         ex_last = sb([P, H], F32, "ex_last")
-        y_rest = sb([P, R - 1, H], F32, "y_rest")
-        y_pl = [ex_win[0][:, H:]] + [y_rest[:, t, :] for t in range(R - 1)]
-        ex_pl = [ex_win[t + 1][:, H:] for t in range(R - 1)] + [ex_last[:]]
-        for t in range(R):
-            acc = project(xa, xa_s, wa_codes, wa_scales, t)
-            nc.scalar.copy(y_win[t][:], acc[:])
-            nc.scalar.copy(y_pl[t], acc[:])
+        y_rest = sb([P, 2 * HALF], F32, "y_rest")
+        y_lo = [sb([P, HALF], F32, "y_lo%d" % t, "y_lo%d" % t)[:] for t in range(R)]
+        y_hi = [ex_win[0][:, H : H + HALF], ex_win[0][:, H + HALF :], y_rest[:, 0:HALF], y_rest[:, HALF:]]
+        y_plain = (y_lo, y_hi)
+        ex_plain = [ex_win[t + 1][:, H:] for t in range(R - 1)] + [ex_last[:]]
 
-        wb_codes, wb_scales = quantise_weight(wb_raw, "wb")
+        for t in range(R):
+            acc = project(xa_codes, xa_scales, wa_codes, wa_scales, t)
+            nc.scalar.copy(y_win[t][:], acc[:])
+            nc.scalar.copy(y_lo[t], acc[:, 0:HALF])
+            nc.sync.dma_start(y_hi[t], y_win[t][:, HALF:])
+            if t == 0:
+                wb_rounded = round_weight(wb_raw, "wb")
 
         def difference(t, lst, u, tag):
             c0, c1 = HALVES[u]
             diff = sb([P, HALF], F32, "%s_%d" % (tag, u), tag)
-            nc.vector.tensor_tensor(diff[:], y_win[t][:].indirect(entries(lst, c0, c1)), y_pl[t][:, c0:c1], ALU.subtract)
+            nc.vector.tensor_tensor(diff[:], y_win[t][:].indirect(entries(lst, c0, c1)), y_plain[u][t], ALU.subtract)
             return diff
+
+        diff1, diff2 = [], []
+        for t in range(R):
+            if t == 1:
+                wb_codes, wb_scales = quantise_weight(wb_rounded, "wb", "y_lo0")
+            diff1.append(difference(t, l_n1, 0, "diff1_%d" % t))
+            diff2.append(difference(t, l_n2, 0, "diff2_%d" % t))
+        w1_scale_bytes = deal(w1_scale_raw, U8, 1, 1, "w1_scale_bytes", "y_lo%d" % (R - 1))
 
         d_win = [sb([P, H], F32, "d_win%d" % t) for t in range(R)]
         for t in range(R):
-            acc = project(xb, xb_s, wb_codes, wb_scales, t)
+            acc = project(xb_codes, xb_scales, wb_codes, wb_scales, t)
             nc.scalar.activation(d_win[t][:], acc[:], ACT.Copy, scale=half_gate[:, t : t + 1])
 
-        nh_win = [sb([P, H], F32, "nh_win%d" % t) for t in range(R)]
-        flat = "p t c -> p (t c)"
+        neg_h_win = [sb([P, H], F32, "neg_h_win%d" % t) for t in range(R)]
 
-        def terms(k, diff1, diff2):
+        def terms(k, by_n1, by_n2):
             c0, c1 = CHUNKS[k]
             part = slice(c0 % HALF, c0 % HALF + c1 - c0)
             term1 = sb([P, R, c1 - c0], F32, "term1_%d" % k)
             term2 = sb([P, R, c1 - c0], F32, "term2_%d" % k)
             for t in range(R):
-                nc.vector.scalar_tensor_tensor(term1[:, t, :], diff1[t][:, part], 2.0, d_win[t][:, c0:c1], ALU.mult, ALU.mult)
+                nc.vector.scalar_tensor_tensor(term1[:, t, :], by_n1[t][:, part], 2.0, d_win[t][:, c0:c1], ALU.mult, ALU.mult)
             for t in range(R):
-                nc.vector.tensor_tensor(term2[:, t, :], d_win[t][:].indirect(entries(l_n3, c0, c1)), diff2[t][:, part], ALU.mult)
+                nc.vector.tensor_tensor(term2[:, t, :], d_win[t][:].indirect(entries(l_n3, c0, c1)), by_n2[t][:, part], ALU.mult)
             return term1, term2
 
         def sum_on_tensor(k, term1, term2):
@@ -180,10 +191,16 @@ def tile_picked_twtflowblse_none_po_kernel(tc, x_words, x_scales, wa, wb, gt, w1
             banks = [psum.tile([P, R, P], F32, name="z_turned", tag="turn", bufs=2) for b0 in starts]
             for t in range(R):
                 for b0, z_turned in zip(starts, banks):
-                    turn_add(z_turned[:, t, :], (term1[:, t, b0 : b0 + P], term2[:, t, b0 : b0 + P]))
+                    for term, first in ((term1, True), (term2, False)):
+                        nc.tensor.matmul(
+                            z_turned[:, t, :], term[:, t, b0 : b0 + P], ident[:], start=first, stop=not first, is_transpose=True
+                        )
             for b0, z_turned in zip(starts, banks):
                 pairs = keep.tile([P, R * P], BF16, name="pairs", bufs=2, align_bytes=64)
-                nc.scalar.copy(pairs[:].rearrange("j (u p e) -> j u p e", u=2, e=2), z_turned[:].rearrange("j (u e) p -> j u p e", u=2))
+                nc.scalar.copy(
+                    pairs[:].rearrange("j (u p e) -> j u p e", u=2, e=2),
+                    z_turned[:].rearrange("j (u e) p -> j u p e", u=2),
+                )
                 back = psum.tile([P, 2, P], F32, name="back", tag="back", bufs=2)
                 for u in range(2):
                     nc.tensor.transpose(back[:, u, :], pairs[:].bitcast(F32)[:, P * u : P * (u + 1)], ident[:])
@@ -191,23 +208,16 @@ def tile_picked_twtflowblse_none_po_kernel(tc, x_words, x_scales, wa, wb, gt, w1
                 nc.scalar.copy(words.rearrange("p (j u) -> p j u", u=2), back[:].rearrange("p u j -> p j u"))
             return z_bf
 
-        def sum_on_vector(k, term1, term2):
-            c0, c1 = CHUNKS[k]
-            z = sb([P, R, c1 - c0], F32, "z%d" % k)
-            nc.vector.tensor_tensor(z[:].rearrange(flat), term1[:].rearrange(flat), term2[:].rearrange(flat), ALU.add)
-            return z
-
         def mix(k, z_bf):
             c0, c1 = CHUNKS[k]
-            w = c1 - c0
-            z_codes = sb([P, w], U32, "z_codes%d" % k)
-            z_scales = sb([P, w], U8, "z_scales%d" % k)
+            z_codes = sb([P, c1 - c0], U32, "z_codes%d" % k)
+            z_scales = sb([P, c1 - c0], U8, "z_scales%d" % k)
             nc.vector.quantize_mx(z_codes[:].bitcast(FP8X4), z_scales[:], z_bf[:])
             for t in range(R):
                 nc.tensor.matmul_mx(
                     h_bank[t][:, c0:c1],
-                    lhsT=w1w_d[:, 2 * P * t : 2 * P * (t + 1)].bitcast(FP4X4),
-                    lhsT_scale=w1s_d[:, P * t : P * (t + 1)],
+                    lhsT=w1_codes[:, 2 * P * t : 2 * P * (t + 1)].bitcast(FP4X4),
+                    lhsT_scale=w1_scale_bytes[:, P * t : P * (t + 1)],
                     rhs=z_codes[:].bitcast(FP8X4),
                     rhs_scale=z_scales[:],
                     start=True,
@@ -215,73 +225,71 @@ def tile_picked_twtflowblse_none_po_kernel(tc, x_words, x_scales, wa, wb, gt, w1
                 )
                 nc.scalar.activation(ex_win[t][:, c0:c1], h_bank[t][:, c0:c1], ACT.Exp)
                 if k == 0:
-                    nc.sync.dma_start(ex_pl[t][:, c0:c1], ex_win[t][:, c0:c1])
+                    nc.sync.dma_start(ex_plain[t][:, c0:c1], ex_win[t][:, c0:c1])
                 else:
-                    nc.scalar.activation(ex_pl[t][:, c0:c1], h_bank[t][:, c0:c1], ACT.Exp)
+                    nc.scalar.activation(ex_plain[t][:, c0:c1], h_bank[t][:, c0:c1], ACT.Exp)
 
-        h_bank = [psum.tile([P, H], F32, name="h_bank%d" % t, tag="wide", bufs=4) for t in range(R)]
-        diff1, diff2 = [], []
-        for t in range(R):
-            diff1.append(difference(t, l_n1, 0, "diff1_%d" % t))
-            diff2.append(difference(t, l_n2, 0, "diff2_%d" % t))
-        z_bf0 = sum_on_tensor(0, *terms(0, diff1, diff2))
-        mix(0, z_bf0)
+        h_bank = [psum.tile([P, H], F32, name="h_bank%d" % t, tag="wide", bufs=R) for t in range(R)]
+        mix(0, sum_on_tensor(0, *terms(0, diff1, diff2)))
+
         diff1, diff2 = [], []
         for t in range(R):
             diff1.append(difference(t, l_n1, 1, "diff1_%d" % t))
             diff2.append(difference(t, l_n2, 1, "diff2_%d" % t if t < R - 1 else "z_slot0"))
-        mid_terms = terms(1, diff1, diff2)
-        z_bf1 = sum_on_tensor(1, *mid_terms)
-        last_terms = terms(2, diff1, diff2)
-        z_last = sum_on_vector(2, *last_terms)
-        mix(1, z_bf1)
-        z_bf2 = sb([P, R * P], BF16, "z_bf2", "z_slot1")
-        interleave(nc.vector.tensor_copy, z_bf2[:], z_last[:])
-        mix(2, z_bf2)
+        z_bf_mid = sum_on_tensor(1, *terms(1, diff1, diff2))
+
+        term1_last, term2_last = terms(2, diff1, diff2)
+        z_last = sb([P, R, P], F32, "z_last")
+        flat = "p t c -> p (t c)"
+        nc.vector.tensor_tensor(z_last[:].rearrange(flat), term1_last[:].rearrange(flat), term2_last[:].rearrange(flat), ALU.add)
+        mix(1, z_bf_mid)
+        z_bf_last = sb([P, R * P], BF16, "z_bf_last", "z_slot1")
+        round_rows(nc.vector.tensor_copy, z_bf_last[:], z_last[:])
+        mix(2, z_bf_last)
 
         sums, logs = [], []
         for t in range(R):
-            nc.scalar.activation(nh_win[t][:], h_bank[t][:], ACT.Copy, scale=-1.0)
+            nc.scalar.activation(neg_h_win[t][:], h_bank[t][:], ACT.Copy, scale=-1.0)
             both = sb([P, H], F32, "both%d" % t)
-            nc.vector.tensor_tensor(both[:], ex_win[t][:].indirect(l_n4[:]), ex_pl[t], ALU.add)
-            lg = sb([P, H], F32, "lg%d" % t)
-            nc.scalar.activation(lg[:, 0:HALF], both[:, 0:HALF], ACT.Ln)
+            nc.vector.tensor_tensor(both[:], ex_win[t][:].indirect(l_n4[:]), ex_plain[t], ALU.add)
+            log_both = sb([P, H], F32, "log_both%d" % t)
+            nc.scalar.activation(log_both[:, 0:HALF], both[:, 0:HALF], ACT.Ln)
             sums.append(both)
-            logs.append(lg)
+            logs.append(log_both)
         for t in range(R):
             nc.scalar.activation(logs[t][:, HALF:], sums[t][:, HALF:], ACT.Ln)
 
-        o_scales = sb([P, H], U8, "o_scales")
-        o_codes = sb([P, H], U32, "o_codes")
+        out_scales = sb([P, H], U8, "out_scales")
+        out_codes = sb([P, H], U32, "out_codes")
         out_rows = out_0.rearrange("(p t) c -> p t c", t=R)
         out_words = out_1[0].rearrange("p c t -> p (c t)").bitcast(I32)
 
         def finish(k):
             c0, c1 = CHUNKS[k]
-            o = sb([P, R, c1 - c0], F32, "o%d" % k)
+            result = sb([P, R, c1 - c0], F32, "result%d" % k)
             for t in range(R):
-                nc.vector.tensor_tensor(o[:, t, :], nh_win[t][:].indirect(entries(l_n5, c0, c1)), logs[t][:, c0:c1], ALU.add)
-            nc.sync.dma_start(out_rows[:, :, c0:c1], o[:])
-            return o
+                nc.vector.tensor_tensor(result[:, t, :], neg_h_win[t][:].indirect(entries(l_n5, c0, c1)), logs[t][:, c0:c1], ALU.add)
+            nc.sync.dma_start(out_rows[:, :, c0:c1], result[:])
+            return result
 
-        def round_out(k, o, engine_copy):
+        def round_result(k, result, engine_copy):
             c0, c1 = CHUNKS[k]
-            o_bf = sb([P, R * (c1 - c0)], BF16, "o_bf%d" % k)
-            interleave(engine_copy, o_bf[:], o[:])
-            return o_bf
+            result_bf = sb([P, R * (c1 - c0)], BF16, "result_bf%d" % k)
+            round_rows(engine_copy, result_bf[:], result[:])
+            return result_bf
 
-        def planes(k, o_bf):
+        def quantise_result(k, result_bf):
             c0, c1 = CHUNKS[k]
-            nc.vector.quantize_mx(o_codes[:, c0:c1].bitcast(FP8X4), o_scales[:, c0:c1], o_bf[:])
-            nc.sync.dma_start(out_words[:, c0:c1], o_codes[:, c0:c1].bitcast(I32))
+            nc.vector.quantize_mx(out_codes[:, c0:c1].bitcast(FP8X4), out_scales[:, c0:c1], result_bf[:])
+            nc.sync.dma_start(out_words[:, c0:c1], out_codes[:, c0:c1].bitcast(I32))
 
-        o_bf0 = round_out(0, finish(0), nc.scalar.copy)
-        o_bf1 = round_out(1, finish(1), nc.scalar.copy)
-        o_last = finish(2)
-        planes(0, o_bf0)
-        o_bf2 = round_out(2, o_last, nc.vector.tensor_copy)
-        planes(1, o_bf1)
-        planes(2, o_bf2)
-        for q in range(4):
+        result_bf_first = round_result(0, finish(0), nc.scalar.copy)
+        result_bf_mid = round_result(1, finish(1), nc.scalar.copy)
+        result_last = finish(2)
+        quantise_result(0, result_bf_first)
+        result_bf_last = round_result(2, result_last, nc.vector.tensor_copy)
+        quantise_result(1, result_bf_mid)
+        quantise_result(2, result_bf_last)
+        for q in range(QUADRANTS):
             queue = nc.scalar if q % 2 else nc.sync
-            queue.dma_start(out_2[0, 4 * q : 4 * q + 4, :].bitcast(I32), o_scales[32 * q : 32 * q + 4, :].bitcast(I32))
+            queue.dma_start(out_2[0, 4 * q : 4 * q + 4, :].bitcast(I32), out_scales[32 * q : 32 * q + 4, :].bitcast(I32))

from contextlib import ExitStack

import concourse.mybir as mybir
from concourse.masks import make_identity

T, S, N, H = 2048, 512, 512, 512
FLOPS = 3 * 2 * 512 * 512 * 512

F32 = mybir.dt.float32
BF16 = mybir.dt.bfloat16
I32 = mybir.dt.int32
U32 = mybir.dt.uint32
U16 = mybir.dt.uint16
U8 = mybir.dt.uint8
FP8X4 = mybir.dt.float8_e4m3fn_x4
FP4X4 = mybir.dt.float4_e2m1fn_x4
ALU = mybir.AluOpType
ACT = mybir.ActivationFunctionType

P = 128
R = 4
QUADRANTS = 4
PER_COLUMN = 16
LINE = 16
HALF = H // 2
HALVES = ((0, HALF), (HALF, H))
CHUNKS = ((0, HALF), (HALF, H - P), (H - P, H))


def tile_picked_twtflowblse_none_po_kernel(
    tc, x_words, x_scales, wa, wb, gt, w1_words, w1_scales, offs, two, n1, n2, n3, n4, n5, out_0, out_1, out_2
):
    nc = tc.nc

    with ExitStack() as ctx:
        lists = ctx.enter_context(tc.tile_pool(name="lists", bufs=1))
        keep = ctx.enter_context(tc.tile_pool(name="keep", bufs=1))
        psum = ctx.enter_context(tc.psum_pool(name="psum", bufs=1))

        def sb(shape, dtype, name, tag=""):
            return keep.tile(shape, dtype, name=name, tag=tag, align_bytes=64)

        def load_list(src, name):
            tile = lists.tile([P, S // PER_COLUMN], U16, name=name)
            nc.sync.dma_start(tile[:], src)
            return tile

        def entries(lst, c0, c1):
            return lst[:, c0 // PER_COLUMN : c1 // PER_COLUMN]

        def load_scales(queues, src, width, name):
            tile = sb([P, width], U8, name)
            nc.vector.memset(tile[:].bitcast(I32), 0)
            for q in range(QUADRANTS):
                queues[q % 2].dma_start(tile[32 * q : 32 * q + 4, :].bitcast(I32), src[0, 4 * q : 4 * q + 4, :].bitcast(I32))
            return tile

        def load_weight(weight, name):
            raw = sb([P, R, H], F32, name + "_raw")
            nc.sync.dma_start(raw[:], weight.rearrange("(p t) c -> p t c", t=R))
            return raw

        def round_rows(engine_copy, dst, src):
            run = LINE // 4
            engine_copy(dst.rearrange("p (c i t) -> p c t i", i=run, t=R), src.rearrange("p t (c i) -> p c t i", i=run))

        def round_weight(raw, name):
            rounded = sb([P, R * H], BF16, name + "_bf")
            for engine_copy, (c0, c1) in zip((nc.scalar.copy, nc.vector.tensor_copy), HALVES):
                round_rows(engine_copy, rounded[:, R * c0 : R * c1], raw[:, :, c0:c1])
            return rounded

        def quantise_weight(rounded, name, tag=""):
            codes = sb([P, H], U32, name + "_codes")
            scales = sb([P, H], U8, name + "_scales", tag)
            nc.vector.quantize_mx(codes[:].bitcast(FP8X4), scales[:], rounded[:])
            return codes, scales

        x_scale_table = load_scales((nc.scalar, nc.sync), x_scales, T, "x_scale_table")
        l_offs = load_list(offs, "l_offs")
        l_two = load_list(two, "l_two")
        w1_word_raw = sb([P, 2 * N], U8, "w1_word_raw")
        nc.sync.dma_start(w1_word_raw[:].bitcast(I32), w1_words[0].bitcast(I32))
        l_n1 = load_list(n1, "l_n1")
        wa_raw = load_weight(wa, "wa")
        x_word_table = sb([P, T], U32, "x_word_table")
        nc.sync.dma_start(x_word_table[:].bitcast(I32), x_words[0].rearrange("p n t -> p (n t)").bitcast(I32))
        l_n2 = load_list(n2, "l_n2")
        wb_raw = load_weight(wb, "wb")
        gate = sb([P, R], F32, "gate")
        nc.sync.dma_start(gate[:], gt.rearrange("(p t) o -> p (t o)", t=R))
        l_n3 = load_list(n3, "l_n3")
        w1_scale_raw = load_scales((nc.sync, nc.sync), w1_scales, N, "w1_scale_raw")
        l_n4 = load_list(n4, "l_n4")
        l_n5 = load_list(n5, "l_n5")

        def pick(table, lst, dtype, name, tag=""):
            picked = sb([P, S], dtype, name, tag)
            nc.vector.tensor_copy(picked[:], table[:].indirect(lst[:]))
            return picked

        def deal(src, dtype, column_bytes, column_elements, name, tag=""):
            run = LINE // column_bytes
            dealt = sb([P, S * column_elements], dtype, name, tag)
            nc.vector.tensor_copy(
                dealt[:].rearrange("p (t c i b) -> p c t i b", t=R, i=run, b=column_elements),
                src[:].rearrange("p (c i t b) -> p c t i b", t=R, i=run, b=column_elements),
            )
            return dealt

        def project(words, word_scales, codes, scales, t):
            acc = psum.tile([P, H], F32, name="acc", tag="wide", bufs=R)
            nc.tensor.matmul_mx(
                acc[:],
                lhsT=words[:, P * t : P * (t + 1)].bitcast(FP8X4),
                lhsT_scale=word_scales[:, P * t : P * (t + 1)],
                rhs=codes[:].bitcast(FP8X4),
                rhs_scale=scales[:],
                start=True,
                stop=True,
            )
            return acc

        ident = sb([P, P], F32, "ident")
        make_identity(nc, ident[:])

        xa_scale_picked = pick(x_scale_table, l_offs, U8, "xa_scale_picked")
        xb_scale_picked = pick(x_scale_table, l_two, U8, "xb_scale_picked")
        xa_scales = deal(xa_scale_picked, U8, 1, 1, "xa_scales")
        xb_scales = deal(xb_scale_picked, U8, 1, 1, "xb_scales")
        w1_codes = deal(w1_word_raw, U8, 2, 2, "w1_codes")
        wa_codes, wa_scales = quantise_weight(round_weight(wa_raw, "wa"), "wa")
        xa_codes = deal(pick(x_word_table, l_offs, U32, "xa_word_picked", "picked"), U32, 4, 1, "xa_codes")
        xb_codes = deal(pick(x_word_table, l_two, U32, "xb_word_picked", "picked"), U32, 4, 1, "xb_codes")
        half_gate = sb([P, R], F32, "half_gate")
        nc.gpsimd.tensor_scalar(half_gate[:], gate[:], 0.5, 0.0, ALU.mult, ALU.add)

        y_win = [sb([P, H], F32, "y_win%d" % t) for t in range(R)]
        ex_win = [sb([P, 2 * H], F32, "ex_win%d" % t) for t in range(R)]
        ex_last = sb([P, H], F32, "ex_last")
        y_rest = sb([P, 2 * HALF], F32, "y_rest")
        y_lo = [sb([P, HALF], F32, "y_lo%d" % t, "y_lo%d" % t)[:] for t in range(R)]
        y_hi = [ex_win[0][:, H : H + HALF], ex_win[0][:, H + HALF :], y_rest[:, 0:HALF], y_rest[:, HALF:]]
        y_plain = (y_lo, y_hi)
        ex_plain = [ex_win[t + 1][:, H:] for t in range(R - 1)] + [ex_last[:]]

        for t in range(R):
            acc = project(xa_codes, xa_scales, wa_codes, wa_scales, t)
            nc.scalar.copy(y_win[t][:], acc[:])
            nc.scalar.copy(y_lo[t], acc[:, 0:HALF])
            nc.sync.dma_start(y_hi[t], y_win[t][:, HALF:])
            if t == 0:
                wb_rounded = round_weight(wb_raw, "wb")

        def difference(t, lst, u, tag):
            c0, c1 = HALVES[u]
            diff = sb([P, HALF], F32, "%s_%d" % (tag, u), tag)
            nc.vector.tensor_tensor(diff[:], y_win[t][:].indirect(entries(lst, c0, c1)), y_plain[u][t], ALU.subtract)
            return diff

        diff1, diff2 = [], []
        for t in range(R):
            if t == 1:
                wb_codes, wb_scales = quantise_weight(wb_rounded, "wb", "y_lo0")
            diff1.append(difference(t, l_n1, 0, "diff1_%d" % t))
            diff2.append(difference(t, l_n2, 0, "diff2_%d" % t))
        w1_scale_bytes = deal(w1_scale_raw, U8, 1, 1, "w1_scale_bytes", "y_lo%d" % (R - 1))

        d_win = [sb([P, H], F32, "d_win%d" % t) for t in range(R)]
        for t in range(R):
            acc = project(xb_codes, xb_scales, wb_codes, wb_scales, t)
            nc.scalar.activation(d_win[t][:], acc[:], ACT.Copy, scale=half_gate[:, t : t + 1])

        neg_h_win = [sb([P, H], F32, "neg_h_win%d" % t) for t in range(R)]

        def terms(k, by_n1, by_n2):
            c0, c1 = CHUNKS[k]
            part = slice(c0 % HALF, c0 % HALF + c1 - c0)
            term1 = sb([P, R, c1 - c0], F32, "term1_%d" % k)
            term2 = sb([P, R, c1 - c0], F32, "term2_%d" % k)
            for t in range(R):
                nc.vector.scalar_tensor_tensor(term1[:, t, :], by_n1[t][:, part], 2.0, d_win[t][:, c0:c1], ALU.mult, ALU.mult)
            for t in range(R):
                nc.vector.tensor_tensor(term2[:, t, :], d_win[t][:].indirect(entries(l_n3, c0, c1)), by_n2[t][:, part], ALU.mult)
            return term1, term2

        def sum_on_tensor(k, term1, term2):
            c0, c1 = CHUNKS[k]
            z_bf = sb([P, R * (c1 - c0)], BF16, "z_bf%d" % k, "z_slot%d" % k)
            starts = range(0, c1 - c0, P)
            banks = [psum.tile([P, R, P], F32, name="z_turned", tag="turn", bufs=2) for b0 in starts]
            for t in range(R):
                for b0, z_turned in zip(starts, banks):
                    for term, first in ((term1, True), (term2, False)):
                        nc.tensor.matmul(
                            z_turned[:, t, :], term[:, t, b0 : b0 + P], ident[:], start=first, stop=not first, is_transpose=True
                        )
            for b0, z_turned in zip(starts, banks):
                pairs = keep.tile([P, R * P], BF16, name="pairs", bufs=2, align_bytes=64)
                nc.scalar.copy(
                    pairs[:].rearrange("j (u p e) -> j u p e", u=2, e=2),
                    z_turned[:].rearrange("j (u e) p -> j u p e", u=2),
                )
                back = psum.tile([P, 2, P], F32, name="back", tag="back", bufs=2)
                for u in range(2):
                    nc.tensor.transpose(back[:, u, :], pairs[:].bitcast(F32)[:, P * u : P * (u + 1)], ident[:])
                words = z_bf[:, R * b0 : R * (b0 + P)].bitcast(F32)
                nc.scalar.copy(words.rearrange("p (j u) -> p j u", u=2), back[:].rearrange("p u j -> p j u"))
            return z_bf

        def mix(k, z_bf):
            c0, c1 = CHUNKS[k]
            z_codes = sb([P, c1 - c0], U32, "z_codes%d" % k)
            z_scales = sb([P, c1 - c0], U8, "z_scales%d" % k)
            nc.vector.quantize_mx(z_codes[:].bitcast(FP8X4), z_scales[:], z_bf[:])
            for t in range(R):
                nc.tensor.matmul_mx(
                    h_bank[t][:, c0:c1],
                    lhsT=w1_codes[:, 2 * P * t : 2 * P * (t + 1)].bitcast(FP4X4),
                    lhsT_scale=w1_scale_bytes[:, P * t : P * (t + 1)],
                    rhs=z_codes[:].bitcast(FP8X4),
                    rhs_scale=z_scales[:],
                    start=True,
                    stop=True,
                )
                nc.scalar.activation(ex_win[t][:, c0:c1], h_bank[t][:, c0:c1], ACT.Exp)
                if k == 0:
                    nc.sync.dma_start(ex_plain[t][:, c0:c1], ex_win[t][:, c0:c1])
                else:
                    nc.scalar.activation(ex_plain[t][:, c0:c1], h_bank[t][:, c0:c1], ACT.Exp)

        h_bank = [psum.tile([P, H], F32, name="h_bank%d" % t, tag="wide", bufs=R) for t in range(R)]
        mix(0, sum_on_tensor(0, *terms(0, diff1, diff2)))

        diff1, diff2 = [], []
        for t in range(R):
            diff1.append(difference(t, l_n1, 1, "diff1_%d" % t))
            diff2.append(difference(t, l_n2, 1, "diff2_%d" % t if t < R - 1 else "z_slot0"))
        z_bf_mid = sum_on_tensor(1, *terms(1, diff1, diff2))

        term1_last, term2_last = terms(2, diff1, diff2)
        z_last = sb([P, R, P], F32, "z_last")
        flat = "p t c -> p (t c)"
        nc.vector.tensor_tensor(z_last[:].rearrange(flat), term1_last[:].rearrange(flat), term2_last[:].rearrange(flat), ALU.add)
        mix(1, z_bf_mid)
        z_bf_last = sb([P, R * P], BF16, "z_bf_last", "z_slot1")
        round_rows(nc.vector.tensor_copy, z_bf_last[:], z_last[:])
        mix(2, z_bf_last)

        sums, logs = [], []
        for t in range(R):
            nc.scalar.activation(neg_h_win[t][:], h_bank[t][:], ACT.Copy, scale=-1.0)
            both = sb([P, H], F32, "both%d" % t)
            nc.vector.tensor_tensor(both[:], ex_win[t][:].indirect(l_n4[:]), ex_plain[t], ALU.add)
            log_both = sb([P, H], F32, "log_both%d" % t)
            nc.scalar.activation(log_both[:, 0:HALF], both[:, 0:HALF], ACT.Ln)
            sums.append(both)
            logs.append(log_both)
        for t in range(R):
            nc.scalar.activation(logs[t][:, HALF:], sums[t][:, HALF:], ACT.Ln)

        out_scales = sb([P, H], U8, "out_scales")
        out_codes = sb([P, H], U32, "out_codes")
        out_rows = out_0.rearrange("(p t) c -> p t c", t=R)
        out_words = out_1[0].rearrange("p c t -> p (c t)").bitcast(I32)

        def finish(k):
            c0, c1 = CHUNKS[k]
            result = sb([P, R, c1 - c0], F32, "result%d" % k)
            for t in range(R):
                nc.vector.tensor_tensor(result[:, t, :], neg_h_win[t][:].indirect(entries(l_n5, c0, c1)), logs[t][:, c0:c1], ALU.add)
            nc.sync.dma_start(out_rows[:, :, c0:c1], result[:])
            return result

        def round_result(k, result, engine_copy):
            c0, c1 = CHUNKS[k]
            result_bf = sb([P, R * (c1 - c0)], BF16, "result_bf%d" % k)
            round_rows(engine_copy, result_bf[:], result[:])
            return result_bf

        def quantise_result(k, result_bf):
            c0, c1 = CHUNKS[k]
            nc.vector.quantize_mx(out_codes[:, c0:c1].bitcast(FP8X4), out_scales[:, c0:c1], result_bf[:])
            nc.sync.dma_start(out_words[:, c0:c1], out_codes[:, c0:c1].bitcast(I32))

        result_bf_first = round_result(0, finish(0), nc.scalar.copy)
        result_bf_mid = round_result(1, finish(1), nc.scalar.copy)
        result_last = finish(2)
        quantise_result(0, result_bf_first)
        result_bf_last = round_result(2, result_last, nc.vector.tensor_copy)
        quantise_result(1, result_bf_mid)
        quantise_result(2, result_bf_last)
        for q in range(QUADRANTS):
            queue = nc.scalar if q % 2 else nc.sync
            queue.dma_start(out_2[0, 4 * q : 4 * q + 4, :].bitcast(I32), out_scales[32 * q : 32 * q + 4, :].bitcast(I32))
